import numpy as np
import ml_dtypes


def mxq(x, axis, fmt="e4m3"):
    dtype, down = {"e4m3": (ml_dtypes.float8_e4m3fn, 7), "e5m2": (ml_dtypes.float8_e5m2, 14)}[fmt]
    v = np.moveaxis(np.asarray(x, np.float32).astype(ml_dtypes.bfloat16).astype(np.float64), axis, -1)
    blocks = v.reshape(v.shape[:-1] + (-1, 32))
    amax = np.abs(blocks).max(-1, keepdims=True)
    byte = np.maximum(np.where(amax > 0, np.frexp(amax)[1] - 1 + 127, 0) - down, 1)
    scale = np.exp2(byte - 127.0)
    codes = (blocks / scale).astype(np.float32).astype(dtype).astype(np.float64)
    return np.moveaxis((codes * scale).reshape(v.shape), -1, axis)


WIDE = False


def mx_kscale(k):
    if not WIDE:
        return np.ones(k)
    levels = np.array([10, -10, 5, -5, 0])
    if k % 512:
        return np.exp2(np.random.permutation(np.resize(levels, k // 32))).repeat(32)
    a = np.empty((k // 512, 16))
    for p in range(k // 512):
        a[p, :8] = np.random.permutation(np.resize(levels, 8))
        for g in range(8):
            far = levels[np.abs(levels - a[p, g]) >= 10]
            a[p, g + 8] = far[np.random.randint(len(far))]
    return np.exp2(a.ravel()).repeat(32)


def f64(x):
    return np.asarray(x).astype(np.float64)


def striped8(idx):
    return np.asarray(idx).reshape(8, -1, 16).transpose(0, 2, 1).reshape(128, -1).astype(np.uint16)


def unstriped8(offs):
    return offs.reshape(8, 16, -1).transpose(0, 2, 1).reshape(8, -1).astype(np.int64)


def pick8(x, idx, run):
    r = np.arange(len(x))
    return x[r[:, None], idx[r % (8 * run) // run]]


E2M1 = np.array([0.0, 0.5, 1.0, 1.5, 2.0, 3.0, 4.0, 6.0, -0.0, -0.5, -1.0, -1.5, -2.0, -3.0, -4.0, -6.0])


def pack_weight(w, fmt):
    k, n = w.shape
    w = f64(np.asarray(w, np.float32).astype(ml_dtypes.bfloat16)).reshape(k // 32, 32, n)
    amax = np.abs(w).max(1)
    if fmt == "e4m3":
        byte = np.frexp(amax)[1] - 1 + 127 - 7
    else:
        mant, ex = np.frexp(amax / 6.0)
        byte = np.where(mant > 0.5, ex, ex - 1) + 127
    byte = np.clip(np.where(amax > 0, byte, 1), 1, 254)
    scaled = (w * np.exp2(127.0 - byte)[:, None, :]).reshape(k, n).astype(np.float32)
    by_word = np.ascontiguousarray(scaled.reshape(k // 512, 128, 4, n).transpose(0, 1, 3, 2))
    if fmt == "e4m3":
        words = by_word.astype(ml_dtypes.float8_e4m3fn).view(np.uint8)
    else:
        c = by_word.astype(ml_dtypes.float4_e2m1fn).view(np.uint8) & 0xF
        words = (c[..., 0::2] | (c[..., 1::2] << 4)).reshape(k // 512, 128, 2 * n)
    return np.ascontiguousarray(words), np.ascontiguousarray(byte.astype(np.uint8).reshape(k // 512, 16, n))


def unpack_weight(words, scales, fmt):
    g, _, n = scales.shape
    words = np.ascontiguousarray(words).reshape(g, 128, n, -1)
    if fmt == "e4m3":
        vals = words.view(ml_dtypes.float8_e4m3fn).astype(np.float64)
    else:
        nib = np.empty((g, 128, n, 4), np.uint8)
        nib[..., 0::2] = words & 0xF
        nib[..., 1::2] = words >> 4
        vals = E2M1[nib]
    vals = vals * np.repeat(np.exp2(scales.astype(np.float64) - 127.0), 8, axis=1)[..., None]
    return vals.transpose(0, 1, 3, 2).reshape(g * 512, n)


D, T, U, I, Q = 512, 1024, 1024, 512, 128


def setup_inputs():
    n = np.random.standard_normal
    idx = np.stack([np.random.permutation(T)[:I] for _ in range(8)])
    idx2 = np.stack([np.random.permutation(T)[:I] for _ in range(8)])
    idx3 = np.stack([np.random.permutation(U)[:I] for _ in range(8)])
    idx4 = np.stack([np.random.permutation(U)[:I] for _ in range(8)])
    idx5 = np.stack([np.random.permutation(U)[:I] for _ in range(8)])
    fd = mx_kscale(D)
    keysp = pack_weight(n((D, T)) / fd[:, None], "e4m3")
    notesp = pack_weight(n((D, U)) / fd[:, None], "e2m1")
    return {
        "query": (n((D, Q)) * 1.0 / np.sqrt(D) * fd[:, None]).astype(np.float32),
        "keys_words": keysp[0],
        "keys_scales": keysp[1],
        "notes_words": notesp[0],
        "notes_scales": notesp[1],
        "offs": striped8(idx),
        "offs2": striped8(idx2),
        "offs3": striped8(idx3),
        "offs4": striped8(idx4),
        "offs5": striped8(idx5),
    }


def reference(query, keys_words, keys_scales, notes_words, notes_scales, offs, offs2, offs3, offs4, offs5):
    idx = unstriped8(offs)
    idx2 = unstriped8(offs2)
    idx3 = unstriped8(offs3)
    idx4 = unstriped8(offs4)
    idx5 = unstriped8(offs5)
    keysu = unpack_weight(keys_words, keys_scales, "e4m3")
    notesu = unpack_weight(notes_words, notes_scales, "e2m1")
    queryq = mxq(f64(query), 0, "e4m3")
    a = queryq.T @ keysu
    b = queryq.T @ notesu
    w = pick8(a, idx, 16) + pick8(a, idx2, 16)
    r = w - pick8(b, idx3, 16)
    f1 = np.zeros((Q, U))
    f1[np.arange(Q)[:, None], idx3[np.arange(Q) % 128 // 16]] = r
    bb = b + f1
    y = np.maximum(pick8(bb, idx4, 16), pick8(bb, idx5, 16))
    return y

@@ -1,0 +1,118 @@
+from contextlib import ExitStack
+
+import concourse.mybir as mybir
+
+D, T, U, I, Q = 512, 1024, 1024, 512, 128
+FLOPS = 2 * D * Q * (T + U)
+
+F32 = mybir.dt.float32
+BF16 = mybir.dt.bfloat16
+I32 = mybir.dt.int32
+U32 = mybir.dt.uint32
+U16 = mybir.dt.uint16
+U8 = mybir.dt.uint8
+FP8X4 = mybir.dt.float8_e4m3fn_x4
+FP4X4 = mybir.dt.float4_e2m1fn_x4
+ADD = mybir.AluOpType.add
+MAX = mybir.AluOpType.max
+COPY = mybir.ActivationFunctionType.Copy
+
+P = 128
+PACK = 4
+N = 256
+H = I // 2
+
+
+def tile_attend_tagteam_two_kernel(tc, query, keys_words, keys_scales, notes_words, notes_scales, offs, offs2, offs3, offs4, offs5, out):
+    nc = tc.nc
+    with ExitStack() as ctx:
+        pool = ctx.enter_context(tc.tile_pool(name="held", bufs=1))
+        psum = ctx.enter_context(tc.psum_pool(name="psum", bufs=1))
+
+        key_plane = pool.tile([P, T], U8, align_bytes=64)
+        note_plane = pool.tile([P, U], U8, align_bytes=64)
+        f1 = pool.tile([P, U], F32)
+        nc.vector.memset(key_plane[:].bitcast(U32), 0)
+        nc.vector.memset(note_plane[:].bitcast(U32), 0)
+        nc.vector.memset(f1[:], 0.0)
+
+        q_raw = pool.tile([P, PACK, Q], F32)
+        nc.sync.dma_start(out=q_raw[:], in_=query.rearrange("(p j) q -> p j q", j=PACK))
+        def load_list(src, name):
+            lst = pool.tile([P, I // 16], U16, name=name)
+            nc.sync.dma_start(lst[:], src)
+            return lst
+
+        l2 = load_list(offs2, "l2")
+        for g in range(4):
+            nc.scalar.dma_start(out=key_plane[32 * g : 32 * g + 4, :].bitcast(I32), in_=keys_scales[0][4 * g : 4 * g + 4, :].bitcast(I32))
+        key_words = pool.tile([P, T], U32, align_bytes=64)
+        nc.sync.dma_start(out=key_words[:].bitcast(I32), in_=keys_words[0].rearrange("p n t -> p (n t)").bitcast(I32))
+        note_words = pool.tile([P, 2 * U], U8, align_bytes=64)
+        nc.sync.dma_start(out=note_words[:].bitcast(I32), in_=notes_words[0].bitcast(I32))
+        for g in range(4):
+            nc.sync.dma_start(out=note_plane[32 * g : 32 * g + 4, :].bitcast(I32), in_=notes_scales[0][4 * g : 4 * g + 4, :].bitcast(I32))
+        l1 = load_list(offs, "l1")
+        l3 = load_list(offs3, "l3")
+        l4 = load_list(offs4, "l4")
+        l5 = load_list(offs5, "l5")
+
+        def half(lst, h):
+            return lst[:, h * (H // 16) : (h + 1) * (H // 16)]
+
+        q_bf = pool.tile([P, Q, PACK], BF16, align_bytes=64)
+        q_words = pool.tile([P, Q], U32, align_bytes=64)
+        q_plane = pool.tile([P, Q], U8, align_bytes=64)
+        halves = [slice(0, Q // 2), slice(Q // 2, Q)]
+        for cols in halves:
+            nc.vector.tensor_copy(out=q_bf[:, cols, :].rearrange("p (c i) t -> p c t i", i=4), in_=q_raw[:, :, cols].rearrange("p t (c i) -> p c t i", i=4))
+        for cols in halves:
+            nc.vector.quantize_mx(out=q_words[:, cols].bitcast(FP8X4), scales=q_plane[:, cols], in_=q_bf[:, cols, :].rearrange("p q t -> p (q t)"))
+
+        a = pool.tile([P, T], F32)
+        b = pool.tile([P, U], F32)
+        a_banks = []
+        b_banks = []
+        for j in range(T // N):
+            bank = psum.tile([P, N], F32, name="a_bank%d" % j)
+            nc.tensor.matmul_mx(out=bank[:], lhsT=q_words[:].bitcast(FP8X4), lhsT_scale=q_plane[:], rhs=key_words[:, j * N : (j + 1) * N].bitcast(FP8X4), rhs_scale=key_plane[:, j * N : (j + 1) * N], start=True, stop=True)
+            a_banks.append(bank)
+        for j in range(U // N):
+            bank = psum.tile([P, N], F32, name="b_bank%d" % j)
+            nc.tensor.matmul_mx(out=bank[:], lhsT=q_words[:].bitcast(FP8X4), lhsT_scale=q_plane[:], rhs=note_words[:, 2 * j * N : 2 * (j + 1) * N].bitcast(FP4X4), rhs_scale=note_plane[:, j * N : (j + 1) * N], start=True, stop=True)
+            b_banks.append(bank)
+
+        def leave(eng, dst, banks, j):
+            if eng == "scalar":
+                nc.scalar.activation(dst[:, j * N : (j + 1) * N], banks[j][:], COPY)
+            else:
+                nc.vector.tensor_copy(dst[:, j * N : (j + 1) * N], banks[j][:])
+
+        for j in range(T // N):
+            leave("scalar" if j % 2 == 0 else "vector", a, a_banks, j)
+
+        g2 = [pool.tile([P, H], F32, name="g2_%d" % h) for h in range(2)]
+        w = [pool.tile([P, H], F32, name="w_%d" % h) for h in range(2)]
+        nb = [pool.tile([P, H], F32, name="nb_%d" % h) for h in range(2)]
+
+        for h in range(2):
+            nc.scalar.activation(g2[h][:], a[:].indirect(half(l2, h)), COPY)
+        for j in range(U // N):
+            leave("vector" if j < 3 else "scalar", b, b_banks, j)
+        for h in range(2):
+            nc.vector.tensor_tensor(w[h][:], a[:].indirect(half(l1, h)), g2[h][:], ADD)
+            nc.scalar.activation(nb[h][:], b[:].indirect(half(l3, h)), COPY, scale=-1.0)
+        for h in range(2):
+            nc.vector.tensor_tensor(f1[:].indirect(half(l3, h)), w[h][:], nb[h][:], ADD)
+
+        bb = pool.tile([P, U], F32)
+        nc.vector.tensor_tensor(bb[:], b[:], f1[:], ADD)
+        g4 = [pool.tile([P, H], F32, name="g4_%d" % h) for h in range(2)]
+        g5 = [pool.tile([P, H], F32, name="g5_%d" % h) for h in range(2)]
+        for h in range(2):
+            nc.scalar.activation(g4[h][:], bb[:].indirect(half(l4, h)), COPY)
+            nc.vector.tensor_copy(g5[h][:], bb[:].indirect(half(l5, h)))
+        for h in range(2):
+            y = pool.tile([P, H], F32, name="y_%d" % h)
+            nc.vector.tensor_tensor(y[:], g4[h][:], g5[h][:], MAX)
+            nc.sync.dma_start(out=out[:, h * H : (h + 1) * H], in_=y[:])

@@ -19,8 +19,11 @@ COPY = mybir.ActivationFunctionType.Copy
 
 P = 128
 PACK = 4
+QUADRANTS = 4
 N = 256
+BANKS = T // N
 H = I // 2
+LANES = 16
 
 
 def tile_attend_tagteam_two_kernel(tc, query, keys_words, keys_scales, notes_words, notes_scales, offs, offs2, offs3, offs4, offs5, out):
@@ -32,87 +35,95 @@ def tile_attend_tagteam_two_kernel(tc, query, keys_words, keys_scales, notes_wor
         key_plane = pool.tile([P, T], U8, align_bytes=64)
         note_plane = pool.tile([P, U], U8, align_bytes=64)
         f1 = pool.tile([P, U], F32)
-        nc.vector.memset(key_plane[:].bitcast(U32), 0)
         nc.vector.memset(note_plane[:].bitcast(U32), 0)
+        nc.vector.memset(key_plane[:].bitcast(U32), 0)
         nc.vector.memset(f1[:], 0.0)
 
-        q_raw = pool.tile([P, PACK, Q], F32)
-        nc.sync.dma_start(out=q_raw[:], in_=query.rearrange("(p j) q -> p j q", j=PACK))
         def load_list(src, name):
-            lst = pool.tile([P, I // 16], U16, name=name)
+            lst = pool.tile([P, I // LANES], U16, name=name)
             nc.sync.dma_start(lst[:], src)
             return lst
 
-        l2 = load_list(offs2, "l2")
-        for g in range(4):
-            nc.scalar.dma_start(out=key_plane[32 * g : 32 * g + 4, :].bitcast(I32), in_=keys_scales[0][4 * g : 4 * g + 4, :].bitcast(I32))
-        key_words = pool.tile([P, T], U32, align_bytes=64)
-        nc.sync.dma_start(out=key_words[:].bitcast(I32), in_=keys_words[0].rearrange("p n t -> p (n t)").bitcast(I32))
+        def load_plane(plane, scales):
+            for g in range(QUADRANTS):
+                nc.sync.dma_start(out=plane[32 * g : 32 * g + 4, :].bitcast(I32), in_=scales[0][4 * g : 4 * g + 4, :].bitcast(I32))
+
+        q_raw = pool.tile([P, PACK, Q], F32)
+        nc.sync.dma_start(out=q_raw[:], in_=query.rearrange("(p j) q -> p j q", j=PACK))
+        list3 = load_list(offs3, "list3")
+        load_plane(note_plane, notes_scales)
         note_words = pool.tile([P, 2 * U], U8, align_bytes=64)
         nc.sync.dma_start(out=note_words[:].bitcast(I32), in_=notes_words[0].bitcast(I32))
-        for g in range(4):
-            nc.sync.dma_start(out=note_plane[32 * g : 32 * g + 4, :].bitcast(I32), in_=notes_scales[0][4 * g : 4 * g + 4, :].bitcast(I32))
-        l1 = load_list(offs, "l1")
-        l3 = load_list(offs3, "l3")
-        l4 = load_list(offs4, "l4")
-        l5 = load_list(offs5, "l5")
+        key_words = pool.tile([P, T], U32, align_bytes=64)
+        nc.sync.dma_start(out=key_words[:].bitcast(I32), in_=keys_words[0].rearrange("p n t -> p (n t)").bitcast(I32))
+        load_plane(key_plane, keys_scales)
+        list2 = load_list(offs2, "list2")
+        list1 = load_list(offs, "list1")
+        list4 = load_list(offs4, "list4")
+        list5 = load_list(offs5, "list5")
 
         def half(lst, h):
-            return lst[:, h * (H // 16) : (h + 1) * (H // 16)]
+            return lst[:, h * (H // LANES) : (h + 1) * (H // LANES)]
 
         q_bf = pool.tile([P, Q, PACK], BF16, align_bytes=64)
         q_words = pool.tile([P, Q], U32, align_bytes=64)
         q_plane = pool.tile([P, Q], U8, align_bytes=64)
-        halves = [slice(0, Q // 2), slice(Q // 2, Q)]
-        for cols in halves:
-            nc.vector.tensor_copy(out=q_bf[:, cols, :].rearrange("p (c i) t -> p c t i", i=4), in_=q_raw[:, :, cols].rearrange("p t (c i) -> p c t i", i=4))
-        for cols in halves:
-            nc.vector.quantize_mx(out=q_words[:, cols].bitcast(FP8X4), scales=q_plane[:, cols], in_=q_bf[:, cols, :].rearrange("p q t -> p (q t)"))
+        q_halves = [slice(0, Q // 2), slice(Q // 2, Q)]
+        for rows, cast in zip(q_halves, (nc.scalar.copy, nc.vector.tensor_copy)):
+            cast(q_bf[:, rows, :].rearrange("p (c i) t -> p c t i", i=4), q_raw[:, :, rows].rearrange("p t (c i) -> p c t i", i=4))
+        for rows in q_halves:
+            nc.vector.quantize_mx(out=q_words[:, rows].bitcast(FP8X4), scales=q_plane[:, rows], in_=q_bf[:, rows, :].rearrange("p q t -> p (q t)"))
 
         a = pool.tile([P, T], F32)
         b = pool.tile([P, U], F32)
-        a_banks = []
-        b_banks = []
-        for j in range(T // N):
-            bank = psum.tile([P, N], F32, name="a_bank%d" % j)
-            nc.tensor.matmul_mx(out=bank[:], lhsT=q_words[:].bitcast(FP8X4), lhsT_scale=q_plane[:], rhs=key_words[:, j * N : (j + 1) * N].bitcast(FP8X4), rhs_scale=key_plane[:, j * N : (j + 1) * N], start=True, stop=True)
-            a_banks.append(bank)
-        for j in range(U // N):
-            bank = psum.tile([P, N], F32, name="b_bank%d" % j)
-            nc.tensor.matmul_mx(out=bank[:], lhsT=q_words[:].bitcast(FP8X4), lhsT_scale=q_plane[:], rhs=note_words[:, 2 * j * N : 2 * (j + 1) * N].bitcast(FP4X4), rhs_scale=note_plane[:, j * N : (j + 1) * N], start=True, stop=True)
-            b_banks.append(bank)
 
-        def leave(eng, dst, banks, j):
-            if eng == "scalar":
-                nc.scalar.activation(dst[:, j * N : (j + 1) * N], banks[j][:], COPY)
-            else:
-                nc.vector.tensor_copy(dst[:, j * N : (j + 1) * N], banks[j][:])
+        def cols(j):
+            return slice(j * N, (j + 1) * N)
 
-        for j in range(T // N):
-            leave("scalar" if j % 2 == 0 else "vector", a, a_banks, j)
+        def score(name, words, scales):
+            bank = psum.tile([P, N], F32, name=name)
+            nc.tensor.matmul_mx(out=bank[:], lhsT=q_words[:].bitcast(FP8X4), lhsT_scale=q_plane[:], rhs=words, rhs_scale=scales, start=True, stop=True)
+            return bank
 
-        g2 = [pool.tile([P, H], F32, name="g2_%d" % h) for h in range(2)]
-        w = [pool.tile([P, H], F32, name="w_%d" % h) for h in range(2)]
-        nb = [pool.tile([P, H], F32, name="nb_%d" % h) for h in range(2)]
+        b_banks = [score("b_bank%d" % j, note_words[:, 2 * j * N : 2 * (j + 1) * N].bitcast(FP4X4), note_plane[:, cols(j)]) for j in range(BANKS)]
+        a_banks = [score("a_bank%d" % j, key_words[:, cols(j)].bitcast(FP8X4), key_plane[:, cols(j)]) for j in range(BANKS)]
 
+        def on_scalar(dst, src):
+            nc.scalar.activation(dst, src, COPY)
+
+        for j in range(BANKS):
+            leave = on_scalar if j % 2 == 0 else nc.vector.tensor_copy
+            leave(b[:, cols(j)], b_banks[j][:])
+
+        a2 = [pool.tile([P, H], F32, name="a2_%d" % h) for h in range(2)]
+        part = [pool.tile([P, H], F32, name="part_%d" % h) for h in range(2)]
+        a1_second = pool.tile([P, H], F32)
+        minus_b3 = pool.tile([P, H], F32, name="minus_b3")
+        nc.scalar.activation(minus_b3[:], b[:].indirect(half(list3, 0)), COPY, scale=-1.0)
+        for j in range(BANKS):
+            leave = nc.vector.tensor_copy if j < BANKS - 1 else on_scalar
+            leave(a[:, cols(j)], a_banks[j][:])
+        nc.vector.tensor_tensor(part[0][:], a[:].indirect(half(list1, 0)), minus_b3[:], ADD)
         for h in range(2):
-            nc.scalar.activation(g2[h][:], a[:].indirect(half(l2, h)), COPY)
-        for j in range(U // N):
-            leave("vector" if j < 3 else "scalar", b, b_banks, j)
-        for h in range(2):
-            nc.vector.tensor_tensor(w[h][:], a[:].indirect(half(l1, h)), g2[h][:], ADD)
-            nc.scalar.activation(nb[h][:], b[:].indirect(half(l3, h)), COPY, scale=-1.0)
-        for h in range(2):
-            nc.vector.tensor_tensor(f1[:].indirect(half(l3, h)), w[h][:], nb[h][:], ADD)
+            on_scalar(a2[h][:], a[:].indirect(half(list2, h)))
+        on_scalar(a1_second[:], a[:].indirect(half(list1, 1)))
+        minus_b3 = pool.tile([P, H], F32, name="minus_b3")
+        nc.scalar.activation(minus_b3[:], b[:].indirect(half(list3, 1)), COPY, scale=-1.0)
+        nc.vector.tensor_tensor(f1[:].indirect(half(list3, 0)), part[0][:], a2[0][:], ADD)
+        nc.vector.tensor_tensor(part[1][:], a1_second[:], a2[1][:], ADD)
+        nc.vector.tensor_tensor(f1[:].indirect(half(list3, 1)), part[1][:], minus_b3[:], ADD)
 
         bb = pool.tile([P, U], F32)
-        nc.vector.tensor_tensor(bb[:], b[:], f1[:], ADD)
-        g4 = [pool.tile([P, H], F32, name="g4_%d" % h) for h in range(2)]
-        g5 = [pool.tile([P, H], F32, name="g5_%d" % h) for h in range(2)]
+        for j in range(BANKS - 1):
+            nc.vector.tensor_tensor(bb[:, cols(j)], f1[:, cols(j)], b_banks[j][:], ADD)
+        nc.gpsimd.tensor_tensor(bb[:, cols(BANKS - 1)], f1[:, cols(BANKS - 1)], b[:, cols(BANKS - 1)], ADD)
+
+        bb4 = [pool.tile([P, H], F32, name="bb4_%d" % h) for h in range(2)]
+        bb5 = [pool.tile([P, H], F32, name="bb5_%d" % h) for h in range(2)]
         for h in range(2):
-            nc.scalar.activation(g4[h][:], bb[:].indirect(half(l4, h)), COPY)
-            nc.vector.tensor_copy(g5[h][:], bb[:].indirect(half(l5, h)))
+            on_scalar(bb4[h][:], bb[:].indirect(half(list4, h)))
+            nc.vector.tensor_copy(bb5[h][:], bb[:].indirect(half(list5, h)))
         for h in range(2):
             y = pool.tile([P, H], F32, name="y_%d" % h)
-            nc.vector.tensor_tensor(y[:], g4[h][:], g5[h][:], MAX)
+            nc.vector.tensor_tensor(y[:], bb4[h][:], bb5[h][:], MAX)
             nc.sync.dma_start(out=out[:, h * H : (h + 1) * H], in_=y[:])

from contextlib import ExitStack

import concourse.mybir as mybir

D, T, U, I, Q = 512, 1024, 1024, 512, 128
FLOPS = 2 * D * Q * (T + U)

F32 = mybir.dt.float32
BF16 = mybir.dt.bfloat16
I32 = mybir.dt.int32
U32 = mybir.dt.uint32
U16 = mybir.dt.uint16
U8 = mybir.dt.uint8
FP8X4 = mybir.dt.float8_e4m3fn_x4
FP4X4 = mybir.dt.float4_e2m1fn_x4
ADD = mybir.AluOpType.add
MAX = mybir.AluOpType.max
COPY = mybir.ActivationFunctionType.Copy

P = 128
PACK = 4
QUADRANTS = 4
N = 256
BANKS = T // N
H = I // 2
LANES = 16


def tile_attend_tagteam_two_kernel(tc, query, keys_words, keys_scales, notes_words, notes_scales, offs, offs2, offs3, offs4, offs5, out):
    nc = tc.nc
    with ExitStack() as ctx:
        pool = ctx.enter_context(tc.tile_pool(name="held", bufs=1))
        psum = ctx.enter_context(tc.psum_pool(name="psum", bufs=1))

        key_plane = pool.tile([P, T], U8, align_bytes=64)
        note_plane = pool.tile([P, U], U8, align_bytes=64)
        f1 = pool.tile([P, U], F32)
        nc.vector.memset(note_plane[:].bitcast(U32), 0)
        nc.vector.memset(key_plane[:].bitcast(U32), 0)
        nc.vector.memset(f1[:], 0.0)

        def load_list(src, name):
            lst = pool.tile([P, I // LANES], U16, name=name)
            nc.sync.dma_start(lst[:], src)
            return lst

        def load_plane(plane, scales):
            for g in range(QUADRANTS):
                nc.sync.dma_start(out=plane[32 * g : 32 * g + 4, :].bitcast(I32), in_=scales[0][4 * g : 4 * g + 4, :].bitcast(I32))

        q_raw = pool.tile([P, PACK, Q], F32)
        nc.sync.dma_start(out=q_raw[:], in_=query.rearrange("(p j) q -> p j q", j=PACK))
        list3 = load_list(offs3, "list3")
        load_plane(note_plane, notes_scales)
        note_words = pool.tile([P, 2 * U], U8, align_bytes=64)
        nc.sync.dma_start(out=note_words[:].bitcast(I32), in_=notes_words[0].bitcast(I32))
        key_words = pool.tile([P, T], U32, align_bytes=64)
        nc.sync.dma_start(out=key_words[:].bitcast(I32), in_=keys_words[0].rearrange("p n t -> p (n t)").bitcast(I32))
        load_plane(key_plane, keys_scales)
        list2 = load_list(offs2, "list2")
        list1 = load_list(offs, "list1")
        list4 = load_list(offs4, "list4")
        list5 = load_list(offs5, "list5")

        def half(lst, h):
            return lst[:, h * (H // LANES) : (h + 1) * (H // LANES)]

        q_bf = pool.tile([P, Q, PACK], BF16, align_bytes=64)
        q_words = pool.tile([P, Q], U32, align_bytes=64)
        q_plane = pool.tile([P, Q], U8, align_bytes=64)
        q_halves = [slice(0, Q // 2), slice(Q // 2, Q)]
        for rows, cast in zip(q_halves, (nc.scalar.copy, nc.vector.tensor_copy)):
            cast(q_bf[:, rows, :].rearrange("p (c i) t -> p c t i", i=4), q_raw[:, :, rows].rearrange("p t (c i) -> p c t i", i=4))
        for rows in q_halves:
            nc.vector.quantize_mx(out=q_words[:, rows].bitcast(FP8X4), scales=q_plane[:, rows], in_=q_bf[:, rows, :].rearrange("p q t -> p (q t)"))

        a = pool.tile([P, T], F32)
        b = pool.tile([P, U], F32)

        def cols(j):
            return slice(j * N, (j + 1) * N)

        def score(name, words, scales):
            bank = psum.tile([P, N], F32, name=name)
            nc.tensor.matmul_mx(out=bank[:], lhsT=q_words[:].bitcast(FP8X4), lhsT_scale=q_plane[:], rhs=words, rhs_scale=scales, start=True, stop=True)
            return bank

        b_banks = [score("b_bank%d" % j, note_words[:, 2 * j * N : 2 * (j + 1) * N].bitcast(FP4X4), note_plane[:, cols(j)]) for j in range(BANKS)]
        a_banks = [score("a_bank%d" % j, key_words[:, cols(j)].bitcast(FP8X4), key_plane[:, cols(j)]) for j in range(BANKS)]

        def on_scalar(dst, src):
            nc.scalar.activation(dst, src, COPY)

        for j in range(BANKS):
            leave = on_scalar if j % 2 == 0 else nc.vector.tensor_copy
            leave(b[:, cols(j)], b_banks[j][:])

        a2 = [pool.tile([P, H], F32, name="a2_%d" % h) for h in range(2)]
        part = [pool.tile([P, H], F32, name="part_%d" % h) for h in range(2)]
        a1_second = pool.tile([P, H], F32)
        minus_b3 = pool.tile([P, H], F32, name="minus_b3")
        nc.scalar.activation(minus_b3[:], b[:].indirect(half(list3, 0)), COPY, scale=-1.0)
        for j in range(BANKS):
            leave = nc.vector.tensor_copy if j < BANKS - 1 else on_scalar
            leave(a[:, cols(j)], a_banks[j][:])
        nc.vector.tensor_tensor(part[0][:], a[:].indirect(half(list1, 0)), minus_b3[:], ADD)
        for h in range(2):
            on_scalar(a2[h][:], a[:].indirect(half(list2, h)))
        on_scalar(a1_second[:], a[:].indirect(half(list1, 1)))
        minus_b3 = pool.tile([P, H], F32, name="minus_b3")
        nc.scalar.activation(minus_b3[:], b[:].indirect(half(list3, 1)), COPY, scale=-1.0)
        nc.vector.tensor_tensor(f1[:].indirect(half(list3, 0)), part[0][:], a2[0][:], ADD)
        nc.vector.tensor_tensor(part[1][:], a1_second[:], a2[1][:], ADD)
        nc.vector.tensor_tensor(f1[:].indirect(half(list3, 1)), part[1][:], minus_b3[:], ADD)

        bb = pool.tile([P, U], F32)
        for j in range(BANKS - 1):
            nc.vector.tensor_tensor(bb[:, cols(j)], f1[:, cols(j)], b_banks[j][:], ADD)
        nc.gpsimd.tensor_tensor(bb[:, cols(BANKS - 1)], f1[:, cols(BANKS - 1)], b[:, cols(BANKS - 1)], ADD)

        bb4 = [pool.tile([P, H], F32, name="bb4_%d" % h) for h in range(2)]
        bb5 = [pool.tile([P, H], F32, name="bb5_%d" % h) for h in range(2)]
        for h in range(2):
            on_scalar(bb4[h][:], bb[:].indirect(half(list4, h)))
            nc.vector.tensor_copy(bb5[h][:], bb[:].indirect(half(list5, h)))
        for h in range(2):
            y = pool.tile([P, H], F32, name="y_%d" % h)
            nc.vector.tensor_tensor(y[:], bb4[h][:], bb5[h][:], MAX)
            nc.sync.dma_start(out=out[:, h * H : (h + 1) * H], in_=y[:])
